import numpy as np
import ml_dtypes


def mxq(x, axis, fmt="e4m3"):
    dtype, down = {"e4m3": (ml_dtypes.float8_e4m3fn, 7), "e5m2": (ml_dtypes.float8_e5m2, 14)}[fmt]
    v = np.moveaxis(np.asarray(x, np.float32).astype(ml_dtypes.bfloat16).astype(np.float64), axis, -1)
    blocks = v.reshape(v.shape[:-1] + (-1, 32))
    amax = np.abs(blocks).max(-1, keepdims=True)
    byte = np.maximum(np.where(amax > 0, np.frexp(amax)[1] - 1 + 127, 0) - down, 1)
    scale = np.exp2(byte - 127.0)
    codes = (blocks / scale).astype(np.float32).astype(dtype).astype(np.float64)
    return np.moveaxis((codes * scale).reshape(v.shape), -1, axis)


WIDE = False


def mx_kscale(k):
    if not WIDE:
        return np.ones(k)
    levels = np.array([10, -10, 5, -5, 0])
    if k % 512:
        return np.exp2(np.random.permutation(np.resize(levels, k // 32))).repeat(32)
    a = np.empty((k // 512, 16))
    for p in range(k // 512):
        a[p, :8] = np.random.permutation(np.resize(levels, 8))
        for g in range(8):
            far = levels[np.abs(levels - a[p, g]) >= 10]
            a[p, g + 8] = far[np.random.randint(len(far))]
    return np.exp2(a.ravel()).repeat(32)


def f64(x):
    return np.asarray(x).astype(np.float64)


def striped(idx):
    return np.tile(idx.reshape(-1, 16).T, (8, 1)).astype(np.uint16)


def unstriped(offs):
    return offs[:16].T.reshape(-1).astype(np.int64)


def pack_weight(w):
    k, n = w.shape
    w = f64(np.asarray(w, np.float32).astype(ml_dtypes.bfloat16)).reshape(k // 32, 32, n)
    amax = np.abs(w).max(1)
    byte = np.clip(np.where(amax > 0, np.frexp(amax)[1] - 1 + 127 - 7, 1), 1, 254)
    scaled = (w * np.exp2(127.0 - byte)[:, None, :]).reshape(k, n).astype(np.float32)
    words = np.ascontiguousarray(scaled.reshape(k // 512, 128, 4, n).transpose(0, 1, 3, 2)).astype(ml_dtypes.float8_e4m3fn).view(np.uint8)
    return words, np.ascontiguousarray(byte.astype(np.uint8).reshape(k // 512, 16, n))


def unpack_weight(words, scales):
    g, p, n, _ = words.shape
    vals = np.ascontiguousarray(words).view(ml_dtypes.float8_e4m3fn).astype(np.float64) * np.repeat(np.exp2(scales.astype(np.float64) - 127.0), 8, axis=1)[..., None]
    return vals.transpose(0, 1, 3, 2).reshape(g * 512, n)


def relu(v):
    return np.maximum(v, 0.0)


K, T, S, H, G, R = 512, 1024, 512, 512, 2048, 512


def setup_inputs():
    n = np.random.standard_normal
    s = mx_kscale(K)[:, None]
    u = mx_kscale(H)
    packed_xT = pack_weight(n((K, T)) * s)
    packed_vT = pack_weight(n((H, G)) / np.sqrt(H) / u[:, None])
    return {
        "x_words": packed_xT[0],
        "x_scales": packed_xT[1],
        "w1": (n((K, H)) / np.sqrt(K) / s * u).astype(np.float32),
        "v_words": packed_vT[0],
        "v_scales": packed_vT[1],
        "offs": striped(np.random.permutation(T)[:S]),
        "cand": striped(np.random.permutation(G)[:R]),
    }


def reference(x_words, x_scales, w1, v_words, v_scales, offs, cand):
    v_cand = unpack_weight(v_words, v_scales)[:, unstriped(cand)]
    xq = unpack_weight(x_words, x_scales)[:, unstriped(offs)]
    h = mxq(f64(w1), 0, "e4m3").T @ xq
    y = v_cand.T @ mxq(h, 0, "e4m3")
    lg = 1.5 * (np.log(relu(y) + 0.05))
    top = lg.reshape(len(lg), -1, 4).max(axis=2)
    ex = np.exp(lg - np.repeat(top, 4, axis=1))
    total = ex.reshape(len(ex), -1, 4).sum(axis=2)
    a = ex / np.repeat(total, 4, axis=1)
    asc = a * y
    return asc.reshape(len(asc), -1, 4).sum(axis=2)

@@ -1,0 +1,200 @@
+from contextlib import ExitStack
+
+import concourse.mybir as mybir
+from concourse.masks import make_identity
+
+K, T, S, H, G, R = 512, 1024, 512, 512, 2048, 512
+FLOPS = 2 * K * H * S + 2 * H * R * S
+
+F32 = mybir.dt.float32
+BF16 = mybir.dt.bfloat16
+I32 = mybir.dt.int32
+U32 = mybir.dt.uint32
+U16 = mybir.dt.uint16
+U8 = mybir.dt.uint8
+FP8X4 = mybir.dt.float8_e4m3fn_x4
+ALU = mybir.AluOpType
+ACT = mybir.ActivationFunctionType
+
+P = 128
+PACK = 4
+D = 4
+V = S // D
+HALF = R // 2
+FLOOR = 0.05
+EXP_PAIR = 0x7F807F80
+
+
+def tile_picked_ylabel_lin_p_kernel(tc, x_words, x_scales, w1, v_words, v_scales, offs, cand, out):
+    nc = tc.nc
+    with ExitStack() as ctx:
+        keep = ctx.enter_context(tc.tile_pool(name="keep", bufs=1))
+        psum = ctx.enter_context(tc.psum_pool(name="psum", bufs=1))
+
+        offs_sb = keep.tile([P, S // 16], U16, name="offs_sb")
+        cand_sb = keep.tile([P, R // 16], U16, name="cand_sb")
+        x_tab = keep.tile([P, T], U32, name="x_tab", align_bytes=64)
+        xs_tab = keep.tile([P, T], U8, name="xs_tab", align_bytes=64)
+        v_tab = keep.tile([P, G], U32, name="v_tab", align_bytes=64)
+        vs_tab = keep.tile([P, G], U8, name="vs_tab", align_bytes=64)
+        w_raw = [keep.tile([P, PACK, H // 2], F32, name=f"w_raw{u}", align_bytes=64) for u in range(2)]
+        ident = keep.tile([P, P], F32, name="ident", align_bytes=64)
+        one = keep.tile([P, 1], F32, name="one")
+        warm = keep.tile([P, 1], F32, name="warm")
+
+        nc.vector.memset(xs_tab[:].bitcast(I32), 0)
+        nc.vector.memset(one[:], 1.0)
+        nc.vector.memset(vs_tab[:].bitcast(I32), 0)
+
+        nc.sync.dma_start(offs_sb[:], offs)
+        nc.sync.dma_start(x_tab[:].bitcast(I32), x_words[0].rearrange("p n t -> p (n t)").bitcast(I32))
+        for q in range(4):
+            nc.sync.dma_start(xs_tab[32 * q : 32 * q + 4, :].bitcast(I32), x_scales[0, 4 * q : 4 * q + 4, :].bitcast(I32))
+        w_rows = w1.rearrange("(p j) c -> p j c", j=PACK)
+        for u in range(2):
+            nc.sync.dma_start(w_raw[u][:], w_rows[:, :, u * (H // 2) : (u + 1) * (H // 2)])
+        nc.sync.dma_start(cand_sb[:], cand)
+        for q in range(4):
+            nc.sync.dma_start(vs_tab[32 * q : 32 * q + 4, :].bitcast(I32), v_scales[0, 4 * q : 4 * q + 4, :].bitcast(I32))
+        nc.sync.dma_start(v_tab[:].bitcast(I32), v_words[0].rearrange("p n t -> p (n t)").bitcast(I32))
+        make_identity(nc, ident[:])
+        nc.scalar.activation(warm[:], one[:], ACT.Abs_reciprocal_sqrt)
+
+        xg = keep.tile([P, S], U32, name="xg", align_bytes=64)
+        xsg = keep.tile([P, S], U8, name="xsg", align_bytes=64)
+        nc.vector.tensor_copy(xg[:], x_tab[:].indirect(offs_sb[:]))
+        nc.vector.tensor_copy(xsg[:], xs_tab[:].indirect(offs_sb[:]))
+
+        w_bf = keep.tile([P, PACK, P, PACK], BF16, name="w_bf", align_bytes=64)
+        for u in range(2):
+            dst = w_bf[:, :, u * 64 : (u + 1) * 64, :].rearrange("p t m j -> p m j t")
+            src = w_raw[u][:].rearrange("p j (m t) -> p m j t", t=PACK)
+            if u == 0:
+                nc.scalar.copy(dst, src)
+            else:
+                nc.vector.tensor_copy(dst, src)
+        wq = keep.tile([P, H], U32, name="wq", align_bytes=64)
+        wsq = keep.tile([P, H], U8, name="wsq", align_bytes=64)
+        nc.vector.quantize_mx(out=wq[:].bitcast(FP8X4), scales=wsq[:], in_=w_bf[:].rearrange("p t m j -> p (t m j)"))
+
+        h_bf = keep.tile([P, D, V, PACK], BF16, name="h_bf", align_bytes=64)
+        for c in range(4):
+            hb = psum.tile([P, PACK, P], F32, name=f"hb{c}", tag=f"low{c}")
+            cols = slice(c * P, (c + 1) * P)
+            for t in range(PACK):
+                ch = slice(t * P, (t + 1) * P)
+                nc.tensor.matmul_mx(out=hb[:, t, :], lhsT=wq[:, ch].bitcast(FP8X4), lhsT_scale=wsq[:, ch],
+                                    rhs=xg[:, cols].bitcast(FP8X4), rhs_scale=xsg[:, cols], start=True, stop=True)
+            dst = h_bf[:, :, 32 * c : 32 * (c + 1), :]
+            src = hb[:].rearrange("p t (v d) -> p d v t", d=D)
+            if c == 0:
+                nc.vector.tensor_copy(dst, src)
+            else:
+                nc.scalar.copy(dst, src)
+
+        vg = [keep.tile([P, HALF], U32, name=f"vg{u}", align_bytes=64) for u in range(2)]
+        vsg = [keep.tile([P, HALF], U8, name=f"vsg{u}", align_bytes=64) for u in range(2)]
+
+        def gather_v(u):
+            lst = cand_sb[:, u * (HALF // 16) : (u + 1) * (HALF // 16)]
+            nc.vector.tensor_copy(vg[u][:], v_tab[:].indirect(lst))
+            nc.vector.tensor_copy(vsg[u][:], vs_tab[:].indirect(lst))
+
+        gather_v(0)
+        hq = keep.tile([P, S], U32, name="hq", align_bytes=64)
+        hsq = keep.tile([P, S], U8, name="hsq", align_bytes=64)
+        nc.vector.quantize_mx(out=hq[:].bitcast(FP8X4), scales=hsq[:], in_=h_bf[:].rearrange("p d v t -> p (d v t)"))
+        gather_v(1)
+
+        y = [[psum.tile([P, 2, HALF], F32, name=f"y{u}{e}", tag=f"y{u}{e}") for e in range(2)] for u in range(2)]
+        pos = [keep.tile([P, D, HALF], F32, name=f"pos{u}", align_bytes=64) for u in range(2)]
+        ratio = [keep.tile([P, D, HALF], F32, name=f"ratio{u}", align_bytes=64) for u in range(2)]
+        sq = [keep.tile([P, D, HALF], F32, name=f"sq{u}", align_bytes=64) for u in range(2)]
+        rs = [keep.tile([P, D, HALF], F32, name=f"rs{u}", align_bytes=64) for u in range(2)]
+        wt = [keep.tile([P, D, HALF], F32, name=f"wt{u}", align_bytes=64) for u in range(2)]
+        wy = [keep.tile([P, D, HALF], F32, name=f"wy{u}", align_bytes=64) for u in range(2)]
+
+        top2 = [keep.tile([P, 2, HALF], BF16, name=f"top2{u}", align_bytes=64) for u in range(2)]
+        top = [keep.tile([P, HALF], BF16, name=f"top{u}", align_bytes=64) for u in range(2)]
+        inv = [keep.tile([P, HALF], BF16, name=f"inv{u}", align_bytes=64) for u in range(2)]
+        den2 = [keep.tile([P, 2, V], F32, name=f"den2{u}", align_bytes=64) for u in range(2)]
+        rden = [keep.tile([P, 2, V], F32, name=f"rden{u}", align_bytes=64) for u in range(2)]
+        num_tags = [["low1", "low2"], ["low3", "y00"]]
+        num = [[None, None], [None, None]]
+
+        def pair(e):
+            return slice(2 * e, 2 * e + 2)
+
+        def second_product(u):
+            for d in (2, 3, 0, 1):
+                us = slice(d * V, (d + 1) * V)
+                nc.tensor.matmul_mx(out=y[u][d // 2][:, d % 2, :], lhsT=hq[:, us].bitcast(FP8X4), lhsT_scale=hsq[:, us],
+                                    rhs=vg[u][:].bitcast(FP8X4), rhs_scale=vsg[u][:], start=True, stop=True)
+
+        def relu(u, e):
+            nc.scalar.activation(pos[u][:, pair(e), :], y[u][e][:], ACT.Relu)
+
+        def scale_of_top(u):
+            nc.vector.scalar_tensor_tensor(top2[u][:], y[u][0][:], FLOOR, pos[u][:, 2:4, :], ALU.max, ALU.max)
+            nc.vector.tensor_tensor(top[u][:], top2[u][:, 0, :], top2[u][:, 1, :], ALU.max)
+            nc.vector.tensor_scalar(inv[u][:].bitcast(I32), top[u][:].bitcast(I32), EXP_PAIR, EXP_PAIR, ALU.bitwise_xor, ALU.bitwise_and)
+
+        def normalise(u, e):
+            nc.vector.scalar_tensor_tensor(ratio[u][:, pair(e), :], pos[u][:, pair(e), :], FLOOR,
+                                           inv[u][:].unsqueeze(1).to_broadcast([P, 2, HALF]), ALU.add, ALU.mult)
+            nc.scalar.activation(sq[u][:, pair(e), :], ratio[u][:, pair(e), :], ACT.Square, scale=0.125)
+            nc.scalar.activation(rs[u][:, pair(e), :], ratio[u][:, pair(e), :], ACT.Abs_reciprocal_sqrt)
+
+        def weight(u, e):
+            nc.vector.tensor_tensor(wt[u][:, pair(e), :], sq[u][:, pair(e), :], rs[u][:, pair(e), :], ALU.mult)
+
+        def add_turned(dst, src, b, d, first, last):
+            nc.tensor.matmul(dst, lhsT=src[:, d, b * P : (b + 1) * P], rhs=ident[:], is_transpose=True, start=first, stop=last)
+
+        def total(u):
+            den = psum.tile([P, 2, V], F32, name=f"den{u}", tag="low0")
+            for b in range(2):
+                for d in range(D):
+                    add_turned(den[:, b, :], wt[u], b, d, d == 0, d == D - 1)
+            nc.scalar.activation(den2[u][:], den[:], ACT.Square)
+            nc.scalar.activation(rden[u][:], den2[u][:], ACT.Abs_reciprocal_sqrt)
+
+        def weighted(u, e, first):
+            nc.vector.tensor_tensor(wy[u][:, pair(e), :], wt[u][:, pair(e), :], y[u][e][:], ALU.mult)
+            for b in range(2):
+                if first:
+                    num[u][b] = psum.tile([P, V], F32, name=f"num{u}{b}", tag=num_tags[u][b])
+                for i in range(2):
+                    add_turned(num[u][b][:], wy[u], b, 2 * e + i, first and i == 0, (not first) and i == 1)
+
+        def finish(u):
+            for b in range(2):
+                res = keep.tile([P, V], F32, name=f"res{u}{b}", align_bytes=64)
+                nc.vector.tensor_tensor(res[:], num[u][b][:], rden[u][:, b, :], ALU.mult)
+                r0 = u * HALF + b * P
+                nc.sync.dma_start(out[r0 : r0 + P, :], res[:])
+
+        second_product(0)
+        relu(0, 1)
+        relu(0, 0)
+        second_product(1)
+        scale_of_top(0)
+        normalise(0, 1)
+        relu(1, 1)
+        normalise(0, 0)
+        relu(1, 0)
+        scale_of_top(1)
+        weight(0, 1)
+        normalise(1, 1)
+        weight(0, 0)
+        normalise(1, 0)
+        total(0)
+        weighted(0, 0, True)
+        weighted(0, 1, False)
+        weight(1, 1)
+        weight(1, 0)
+        total(1)
+        finish(0)
+        weighted(1, 1, True)
+        weighted(1, 0, False)
+        finish(1)

@@ -35,81 +35,70 @@ def tile_picked_ylabel_lin_p_kernel(tc, x_words, x_scales, w1, v_words, v_scales
         cand_sb = keep.tile([P, R // 16], U16, name="cand_sb")
         x_tab = keep.tile([P, T], U32, name="x_tab", align_bytes=64)
         xs_tab = keep.tile([P, T], U8, name="xs_tab", align_bytes=64)
-        v_tab = keep.tile([P, G], U32, name="v_tab", align_bytes=64)
-        vs_tab = keep.tile([P, G], U8, name="vs_tab", align_bytes=64)
+        v_tab = keep.tile([P, G], U32, name="v_tab", tag="v_then_h", align_bytes=64)
+        vs_tab = keep.tile([P, G], U8, name="vs_tab", tag="vs_then_hs", align_bytes=64)
         w_raw = [keep.tile([P, PACK, H // 2], F32, name=f"w_raw{u}", align_bytes=64) for u in range(2)]
         ident = keep.tile([P, P], F32, name="ident", align_bytes=64)
         one = keep.tile([P, 1], F32, name="one")
         warm = keep.tile([P, 1], F32, name="warm")
 
-        nc.vector.memset(xs_tab[:].bitcast(I32), 0)
+        nc.gpsimd.memset(xs_tab[:].bitcast(I32), 0)
         nc.vector.memset(one[:], 1.0)
-        nc.vector.memset(vs_tab[:].bitcast(I32), 0)
+        nc.gpsimd.memset(vs_tab[:].bitcast(I32), 0)
 
+        w_rows = w1.rearrange("(p j) c -> p j c", j=PACK)
+        nc.scalar.dma_start(w_raw[0][:], w_rows[:, :, 0 : H // 2])
         nc.sync.dma_start(offs_sb[:], offs)
-        nc.sync.dma_start(x_tab[:].bitcast(I32), x_words[0].rearrange("p n t -> p (n t)").bitcast(I32))
         for q in range(4):
             nc.sync.dma_start(xs_tab[32 * q : 32 * q + 4, :].bitcast(I32), x_scales[0, 4 * q : 4 * q + 4, :].bitcast(I32))
-        w_rows = w1.rearrange("(p j) c -> p j c", j=PACK)
-        for u in range(2):
-            nc.sync.dma_start(w_raw[u][:], w_rows[:, :, u * (H // 2) : (u + 1) * (H // 2)])
+        nc.sync.dma_start(w_raw[1][:], w_rows[:, :, H // 2 : H])
+        nc.sync.dma_start(x_tab[:].bitcast(I32), x_words[0].rearrange("p n t -> p (n t)").bitcast(I32))
         nc.sync.dma_start(cand_sb[:], cand)
         for q in range(4):
             nc.sync.dma_start(vs_tab[32 * q : 32 * q + 4, :].bitcast(I32), v_scales[0, 4 * q : 4 * q + 4, :].bitcast(I32))
         nc.sync.dma_start(v_tab[:].bitcast(I32), v_words[0].rearrange("p n t -> p (n t)").bitcast(I32))
         make_identity(nc, ident[:])
-        nc.scalar.activation(warm[:], one[:], ACT.Abs_reciprocal_sqrt)
+        nc.scalar.activation(warm[:], one[:], ACT.Sqrt)
 
-        xg = keep.tile([P, S], U32, name="xg", align_bytes=64)
         xsg = keep.tile([P, S], U8, name="xsg", align_bytes=64)
-        nc.vector.tensor_copy(xg[:], x_tab[:].indirect(offs_sb[:]))
         nc.vector.tensor_copy(xsg[:], xs_tab[:].indirect(offs_sb[:]))
 
-        w_bf = keep.tile([P, PACK, P, PACK], BF16, name="w_bf", align_bytes=64)
-        for u in range(2):
-            dst = w_bf[:, :, u * 64 : (u + 1) * 64, :].rearrange("p t m j -> p m j t")
-            src = w_raw[u][:].rearrange("p j (m t) -> p m j t", t=PACK)
-            if u == 0:
-                nc.scalar.copy(dst, src)
-            else:
-                nc.vector.tensor_copy(dst, src)
+        w_bf = keep.tile([P, PACK, P, PACK], BF16, name="w_bf", tag="w_then_x", align_bytes=64)
+        for m0, m1, engine_copy in ((0, 64, nc.scalar.copy), (64, 80, nc.scalar.copy), (80, 128, nc.vector.tensor_copy)):
+            u = m0 // 64
+            dst = w_bf[:, :, m0:m1, :].rearrange("p t m j -> p m j t")
+            src = w_raw[u][:].rearrange("p j (m t) -> p m j t", t=PACK)[:, m0 - 64 * u : m1 - 64 * u, :, :]
+            engine_copy(dst, src)
         wq = keep.tile([P, H], U32, name="wq", align_bytes=64)
         wsq = keep.tile([P, H], U8, name="wsq", align_bytes=64)
         nc.vector.quantize_mx(out=wq[:].bitcast(FP8X4), scales=wsq[:], in_=w_bf[:].rearrange("p t m j -> p (t m j)"))
 
+        xg = keep.tile([P, S], U32, name="xg", tag="w_then_x", align_bytes=64)
         h_bf = keep.tile([P, D, V, PACK], BF16, name="h_bf", align_bytes=64)
         for c in range(4):
             hb = psum.tile([P, PACK, P], F32, name=f"hb{c}", tag=f"low{c}")
             cols = slice(c * P, (c + 1) * P)
+            nc.vector.tensor_copy(xg[:, cols], x_tab[:].indirect(offs_sb[:, c * (P // 16) : (c + 1) * (P // 16)]))
             for t in range(PACK):
                 ch = slice(t * P, (t + 1) * P)
                 nc.tensor.matmul_mx(out=hb[:, t, :], lhsT=wq[:, ch].bitcast(FP8X4), lhsT_scale=wsq[:, ch],
                                     rhs=xg[:, cols].bitcast(FP8X4), rhs_scale=xsg[:, cols], start=True, stop=True)
-            dst = h_bf[:, :, 32 * c : 32 * (c + 1), :]
-            src = hb[:].rearrange("p t (v d) -> p d v t", d=D)
-            if c == 0:
-                nc.vector.tensor_copy(dst, src)
-            else:
-                nc.scalar.copy(dst, src)
+            nc.scalar.copy(h_bf[:, :, 32 * c : 32 * (c + 1), :], hb[:].rearrange("p t (v d) -> p d v t", d=D))
 
-        vg = [keep.tile([P, HALF], U32, name=f"vg{u}", align_bytes=64) for u in range(2)]
-        vsg = [keep.tile([P, HALF], U8, name=f"vsg{u}", align_bytes=64) for u in range(2)]
-
-        def gather_v(u):
-            lst = cand_sb[:, u * (HALF // 16) : (u + 1) * (HALF // 16)]
-            nc.vector.tensor_copy(vg[u][:], v_tab[:].indirect(lst))
-            nc.vector.tensor_copy(vsg[u][:], vs_tab[:].indirect(lst))
-
-        gather_v(0)
-        hq = keep.tile([P, S], U32, name="hq", align_bytes=64)
-        hsq = keep.tile([P, S], U8, name="hsq", align_bytes=64)
-        nc.vector.quantize_mx(out=hq[:].bitcast(FP8X4), scales=hsq[:], in_=h_bf[:].rearrange("p d v t -> p (d v t)"))
-        gather_v(1)
+        vsg = keep.tile([P, R], U8, name="vsg", align_bytes=64)
+        nc.vector.tensor_copy(vsg[:], vs_tab[:].indirect(cand_sb[:]))
+        vg = keep.tile([P, R], U32, name="vg", align_bytes=64)
+        nc.vector.tensor_copy(vg[:], v_tab[:].indirect(cand_sb[:]))
+        hq = keep.tile([P, S], U32, name="hq", tag="v_then_h", align_bytes=64)
+        hsq = keep.tile([P, S], U8, name="hsq", tag="vs_then_hs", align_bytes=64)
+        for e in (1, 0):
+            us = slice(2 * e * V, (2 * e + 2) * V)
+            nc.vector.quantize_mx(out=hq[:, us].bitcast(FP8X4), scales=hsq[:, us],
+                                  in_=h_bf[:, 2 * e : 2 * e + 2, :, :].rearrange("p d v t -> p (d v t)"))
 
         y = [[psum.tile([P, 2, HALF], F32, name=f"y{u}{e}", tag=f"y{u}{e}") for e in range(2)] for u in range(2)]
         pos = [keep.tile([P, D, HALF], F32, name=f"pos{u}", align_bytes=64) for u in range(2)]
         ratio = [keep.tile([P, D, HALF], F32, name=f"ratio{u}", align_bytes=64) for u in range(2)]
-        sq = [keep.tile([P, D, HALF], F32, name=f"sq{u}", align_bytes=64) for u in range(2)]
         rs = [keep.tile([P, D, HALF], F32, name=f"rs{u}", align_bytes=64) for u in range(2)]
         wt = [keep.tile([P, D, HALF], F32, name=f"wt{u}", align_bytes=64) for u in range(2)]
         wy = [keep.tile([P, D, HALF], F32, name=f"wy{u}", align_bytes=64) for u in range(2)]
@@ -119,7 +108,7 @@ def tile_picked_ylabel_lin_p_kernel(tc, x_words, x_scales, w1, v_words, v_scales
         inv = [keep.tile([P, HALF], BF16, name=f"inv{u}", align_bytes=64) for u in range(2)]
         den2 = [keep.tile([P, 2, V], F32, name=f"den2{u}", align_bytes=64) for u in range(2)]
         rden = [keep.tile([P, 2, V], F32, name=f"rden{u}", align_bytes=64) for u in range(2)]
-        num_tags = [["low1", "low2"], ["low3", "y00"]]
+        num_tags = [["low2", "low3"], ["low0", "low1"]]
         num = [[None, None], [None, None]]
 
         def pair(e):
@@ -129,72 +118,82 @@ def tile_picked_ylabel_lin_p_kernel(tc, x_words, x_scales, w1, v_words, v_scales
             for d in (2, 3, 0, 1):
                 us = slice(d * V, (d + 1) * V)
                 nc.tensor.matmul_mx(out=y[u][d // 2][:, d % 2, :], lhsT=hq[:, us].bitcast(FP8X4), lhsT_scale=hsq[:, us],
-                                    rhs=vg[u][:].bitcast(FP8X4), rhs_scale=vsg[u][:], start=True, stop=True)
+                                    rhs=vg[:, u * HALF : (u + 1) * HALF].bitcast(FP8X4), rhs_scale=vsg[:, u * HALF : (u + 1) * HALF], start=True, stop=True)
 
         def relu(u, e):
             nc.scalar.activation(pos[u][:, pair(e), :], y[u][e][:], ACT.Relu)
 
-        def scale_of_top(u):
+        def top_of_pairs(u):
             nc.vector.scalar_tensor_tensor(top2[u][:], y[u][0][:], FLOOR, pos[u][:, 2:4, :], ALU.max, ALU.max)
+
+        def top_of_four(u):
             nc.vector.tensor_tensor(top[u][:], top2[u][:, 0, :], top2[u][:, 1, :], ALU.max)
+
+        def inverse_scale(u):
             nc.vector.tensor_scalar(inv[u][:].bitcast(I32), top[u][:].bitcast(I32), EXP_PAIR, EXP_PAIR, ALU.bitwise_xor, ALU.bitwise_and)
 
         def normalise(u, e):
             nc.vector.scalar_tensor_tensor(ratio[u][:, pair(e), :], pos[u][:, pair(e), :], FLOOR,
                                            inv[u][:].unsqueeze(1).to_broadcast([P, 2, HALF]), ALU.add, ALU.mult)
-            nc.scalar.activation(sq[u][:, pair(e), :], ratio[u][:, pair(e), :], ACT.Square, scale=0.125)
-            nc.scalar.activation(rs[u][:, pair(e), :], ratio[u][:, pair(e), :], ACT.Abs_reciprocal_sqrt)
+            nc.scalar.activation(rs[u][:, pair(e), :], ratio[u][:, pair(e), :], ACT.Sqrt, scale=1.0 / 256)
+
+        def add_turned(dst, src, b, ds, first, last):
+            for d in ds:
+                nc.tensor.matmul(dst, lhsT=src[:, d, b * P : (b + 1) * P], rhs=ident[:], is_transpose=True,
+                                 start=first and d == ds[0], stop=last and d == ds[-1])
 
         def weight(u, e):
-            nc.vector.tensor_tensor(wt[u][:, pair(e), :], sq[u][:, pair(e), :], rs[u][:, pair(e), :], ALU.mult)
-
-        def add_turned(dst, src, b, d, first, last):
-            nc.tensor.matmul(dst, lhsT=src[:, d, b * P : (b + 1) * P], rhs=ident[:], is_transpose=True, start=first, stop=last)
+            nc.vector.tensor_tensor(wt[u][:, pair(e), :], ratio[u][:, pair(e), :], rs[u][:, pair(e), :], ALU.mult)
 
         def total(u):
-            den = psum.tile([P, 2, V], F32, name=f"den{u}", tag="low0")
+            den = psum.tile([P, 2, V], F32, name=f"den{u}", tag=f"low{u}")
             for b in range(2):
-                for d in range(D):
-                    add_turned(den[:, b, :], wt[u], b, d, d == 0, d == D - 1)
-            nc.scalar.activation(den2[u][:], den[:], ACT.Square)
-            nc.scalar.activation(rden[u][:], den2[u][:], ACT.Abs_reciprocal_sqrt)
+                add_turned(den[:, b, :], wt[u], b, (2, 3, 0, 1), True, True)
+            nc.scalar.activation(den2[u][:], den[:], ACT.Abs_reciprocal_sqrt)
+            nc.scalar.activation(rden[u][:], den2[u][:], ACT.Square)
 
-        def weighted(u, e, first):
-            nc.vector.tensor_tensor(wy[u][:, pair(e), :], wt[u][:, pair(e), :], y[u][e][:], ALU.mult)
-            for b in range(2):
-                if first:
+        def weighted(u, e, blocks):
+            ts = slice(blocks[0] * P, (blocks[-1] + 1) * P)
+            nc.vector.tensor_tensor(wy[u][:, pair(e), ts], wt[u][:, pair(e), ts], y[u][e][:, :, ts], ALU.mult)
+            for b in blocks:
+                if e == 1:
                     num[u][b] = psum.tile([P, V], F32, name=f"num{u}{b}", tag=num_tags[u][b])
-                for i in range(2):
-                    add_turned(num[u][b][:], wy[u], b, 2 * e + i, first and i == 0, (not first) and i == 1)
+                add_turned(num[u][b][:], wy[u], b, (2 * e, 2 * e + 1), e == 1, e == 0)
 
-        def finish(u):
-            for b in range(2):
-                res = keep.tile([P, V], F32, name=f"res{u}{b}", align_bytes=64)
-                nc.vector.tensor_tensor(res[:], num[u][b][:], rden[u][:, b, :], ALU.mult)
-                r0 = u * HALF + b * P
-                nc.sync.dma_start(out[r0 : r0 + P, :], res[:])
+        def finish(u, b):
+            res = keep.tile([P, V], F32, name=f"res{u}{b}", align_bytes=64)
+            nc.vector.tensor_tensor(res[:], num[u][b][:], rden[u][:, b, :], ALU.mult)
+            r0 = u * HALF + b * P
+            nc.sync.dma_start(out[r0 : r0 + P, :], res[:])
 
         second_product(0)
-        relu(0, 1)
-        relu(0, 0)
         second_product(1)
-        scale_of_top(0)
-        normalise(0, 1)
+        relu(0, 1)
         relu(1, 1)
-        normalise(0, 0)
+        top_of_pairs(0)
+        relu(0, 0)
+        top_of_four(0)
+        top_of_pairs(1)
         relu(1, 0)
-        scale_of_top(1)
-        weight(0, 1)
+        inverse_scale(0)
+        top_of_four(1)
+        normalise(0, 1)
+        inverse_scale(1)
+        normalise(0, 0)
         normalise(1, 1)
-        weight(0, 0)
         normalise(1, 0)
+        weight(0, 1)
+        weight(0, 0)
         total(0)
-        weighted(0, 0, True)
-        weighted(0, 1, False)
         weight(1, 1)
         weight(1, 0)
         total(1)
-        finish(0)
-        weighted(1, 1, True)
-        weighted(1, 0, False)
-        finish(1)
+        weighted(0, 1, (0, 1))
+        weighted(0, 0, (0, 1))
+        weighted(1, 1, (0, 1))
+        finish(0, 0)
+        finish(0, 1)
+        weighted(1, 0, (0,))
+        weighted(1, 0, (1,))
+        finish(1, 0)
+        finish(1, 1)

@@ -36,7 +36,7 @@ def tile_picked_ylabel_lin_p_kernel(tc, x_words, x_scales, w1, v_words, v_scales
         x_tab = keep.tile([P, T], U32, name="x_tab", align_bytes=64)
         xs_tab = keep.tile([P, T], U8, name="xs_tab", align_bytes=64)
         v_tab = keep.tile([P, G], U32, name="v_tab", tag="v_then_h", align_bytes=64)
-        vs_tab = keep.tile([P, G], U8, name="vs_tab", tag="vs_then_hs", align_bytes=64)
+        vs_tab = keep.tile([P, G], U8, name="vs_tab", align_bytes=64)
         w_raw = [keep.tile([P, PACK, H // 2], F32, name=f"w_raw{u}", align_bytes=64) for u in range(2)]
         ident = keep.tile([P, P], F32, name="ident", align_bytes=64)
         one = keep.tile([P, 1], F32, name="one")
@@ -73,28 +73,33 @@ def tile_picked_ylabel_lin_p_kernel(tc, x_words, x_scales, w1, v_words, v_scales
         wsq = keep.tile([P, H], U8, name="wsq", align_bytes=64)
         nc.vector.quantize_mx(out=wq[:].bitcast(FP8X4), scales=wsq[:], in_=w_bf[:].rearrange("p t m j -> p (t m j)"))
 
-        xg = keep.tile([P, S], U32, name="xg", tag="w_then_x", align_bytes=64)
-        h_bf = keep.tile([P, D, V, PACK], BF16, name="h_bf", align_bytes=64)
+        xg_first = keep.tile([P, P], U32, name="xg_first", align_bytes=64)
+        xg_rest = keep.tile([P, S - P], U32, name="xg_rest", tag="w_then_x", align_bytes=64)
+        h_bf = keep.tile([P, D, V, PACK], BF16, name="h_bf", tag="h_then_vs", align_bytes=64)
         for c in range(4):
             hb = psum.tile([P, PACK, P], F32, name=f"hb{c}", tag=f"low{c}")
             cols = slice(c * P, (c + 1) * P)
-            nc.vector.tensor_copy(xg[:, cols], x_tab[:].indirect(offs_sb[:, c * (P // 16) : (c + 1) * (P // 16)]))
+            xg = xg_first[:] if c == 0 else xg_rest[:, (c - 1) * P : c * P]
+            nc.vector.tensor_copy(xg, x_tab[:].indirect(offs_sb[:, c * (P // 16) : (c + 1) * (P // 16)]))
             for t in range(PACK):
                 ch = slice(t * P, (t + 1) * P)
                 nc.tensor.matmul_mx(out=hb[:, t, :], lhsT=wq[:, ch].bitcast(FP8X4), lhsT_scale=wsq[:, ch],
-                                    rhs=xg[:, cols].bitcast(FP8X4), rhs_scale=xsg[:, cols], start=True, stop=True)
+                                    rhs=xg.bitcast(FP8X4), rhs_scale=xsg[:, cols], start=True, stop=True)
             nc.scalar.copy(h_bf[:, :, 32 * c : 32 * (c + 1), :], hb[:].rearrange("p t (v d) -> p d v t", d=D))
 
-        vsg = keep.tile([P, R], U8, name="vsg", align_bytes=64)
-        nc.vector.tensor_copy(vsg[:], vs_tab[:].indirect(cand_sb[:]))
+        vsg = [keep.tile([P, HALF], U8, name="vsg0", align_bytes=64)]
+        nc.vector.tensor_copy(vsg[0][:], vs_tab[:].indirect(cand_sb[:, 0 : HALF // 16]))
         vg = keep.tile([P, R], U32, name="vg", align_bytes=64)
         nc.vector.tensor_copy(vg[:], v_tab[:].indirect(cand_sb[:]))
         hq = keep.tile([P, S], U32, name="hq", tag="v_then_h", align_bytes=64)
-        hsq = keep.tile([P, S], U8, name="hsq", tag="vs_then_hs", align_bytes=64)
+        hsq = keep.tile([P, S], U8, name="hsq", align_bytes=64)
         for e in (1, 0):
             us = slice(2 * e * V, (2 * e + 2) * V)
             nc.vector.quantize_mx(out=hq[:, us].bitcast(FP8X4), scales=hsq[:, us],
                                   in_=h_bf[:, 2 * e : 2 * e + 2, :, :].rearrange("p d v t -> p (d v t)"))
+
+        vsg.append(keep.tile([P, HALF], U8, name="vsg1", tag="h_then_vs", align_bytes=64))
+        nc.vector.tensor_copy(vsg[1][:], vs_tab[:].indirect(cand_sb[:, HALF // 16 : R // 16]))
 
         y = [[psum.tile([P, 2, HALF], F32, name=f"y{u}{e}", tag=f"y{u}{e}") for e in range(2)] for u in range(2)]
         pos = [keep.tile([P, D, HALF], F32, name=f"pos{u}", align_bytes=64) for u in range(2)]
@@ -108,8 +113,8 @@ def tile_picked_ylabel_lin_p_kernel(tc, x_words, x_scales, w1, v_words, v_scales
         inv = [keep.tile([P, HALF], BF16, name=f"inv{u}", align_bytes=64) for u in range(2)]
         den2 = [keep.tile([P, 2, V], F32, name=f"den2{u}", align_bytes=64) for u in range(2)]
         rden = [keep.tile([P, 2, V], F32, name=f"rden{u}", align_bytes=64) for u in range(2)]
-        num_tags = [["low2", "low3"], ["low0", "low1"]]
-        num = [[None, None], [None, None]]
+        den = {}
+        num = {}
 
         def pair(e):
             return slice(2 * e, 2 * e + 2)
@@ -118,7 +123,7 @@ def tile_picked_ylabel_lin_p_kernel(tc, x_words, x_scales, w1, v_words, v_scales
             for d in (2, 3, 0, 1):
                 us = slice(d * V, (d + 1) * V)
                 nc.tensor.matmul_mx(out=y[u][d // 2][:, d % 2, :], lhsT=hq[:, us].bitcast(FP8X4), lhsT_scale=hsq[:, us],
-                                    rhs=vg[:, u * HALF : (u + 1) * HALF].bitcast(FP8X4), rhs_scale=vsg[:, u * HALF : (u + 1) * HALF], start=True, stop=True)
+                                    rhs=vg[:, u * HALF : (u + 1) * HALF].bitcast(FP8X4), rhs_scale=vsg[u][:], start=True, stop=True)
 
         def relu(u, e):
             nc.scalar.activation(pos[u][:, pair(e), :], y[u][e][:], ACT.Relu)
@@ -144,12 +149,14 @@ def tile_picked_ylabel_lin_p_kernel(tc, x_words, x_scales, w1, v_words, v_scales
 
         def weight(u, e):
             nc.vector.tensor_tensor(wt[u][:, pair(e), :], ratio[u][:, pair(e), :], rs[u][:, pair(e), :], ALU.mult)
-
-        def total(u):
-            den = psum.tile([P, 2, V], F32, name=f"den{u}", tag=f"low{u}")
             for b in range(2):
-                add_turned(den[:, b, :], wt[u], b, (2, 3, 0, 1), True, True)
-            nc.scalar.activation(den2[u][:], den[:], ACT.Abs_reciprocal_sqrt)
+                if e == 1:
+                    den[u, b] = psum.tile([P, V], F32, name=f"den{u}{b}", tag=f"low{2 * u + b}")
+                add_turned(den[u, b][:], wt[u], b, (2 * e, 2 * e + 1), e == 1, e == 0)
+
+        def invert_total(u):
+            for b in range(2):
+                nc.scalar.activation(den2[u][:, b, :], den[u, b][:], ACT.Abs_reciprocal_sqrt)
             nc.scalar.activation(rden[u][:], den2[u][:], ACT.Square)
 
         def weighted(u, e, blocks):
@@ -157,12 +164,12 @@ def tile_picked_ylabel_lin_p_kernel(tc, x_words, x_scales, w1, v_words, v_scales
             nc.vector.tensor_tensor(wy[u][:, pair(e), ts], wt[u][:, pair(e), ts], y[u][e][:, :, ts], ALU.mult)
             for b in blocks:
                 if e == 1:
-                    num[u][b] = psum.tile([P, V], F32, name=f"num{u}{b}", tag=num_tags[u][b])
-                add_turned(num[u][b][:], wy[u], b, (2 * e, 2 * e + 1), e == 1, e == 0)
+                    num[u, b] = psum.tile([P, V], F32, name=f"num{u}{b}", tag=f"low{2 * u + b}")
+                add_turned(num[u, b][:], wy[u], b, (2 * e, 2 * e + 1), e == 1, e == 0)
 
         def finish(u, b):
             res = keep.tile([P, V], F32, name=f"res{u}{b}", align_bytes=64)
-            nc.vector.tensor_tensor(res[:], num[u][b][:], rden[u][:, b, :], ALU.mult)
+            nc.vector.tensor_tensor(res[:], num[u, b][:], rden[u][:, b, :], ALU.mult)
             r0 = u * HALF + b * P
             nc.sync.dma_start(out[r0 : r0 + P, :], res[:])
 
@@ -184,10 +191,10 @@ def tile_picked_ylabel_lin_p_kernel(tc, x_words, x_scales, w1, v_words, v_scales
         normalise(1, 0)
         weight(0, 1)
         weight(0, 0)
-        total(0)
+        invert_total(0)
         weight(1, 1)
         weight(1, 0)
-        total(1)
+        invert_total(1)
         weighted(0, 1, (0, 1))
         weighted(0, 0, (0, 1))
         weighted(1, 1, (0, 1))

from contextlib import ExitStack

import concourse.mybir as mybir
from concourse.masks import make_identity

K, T, S, H, G, R = 512, 1024, 512, 512, 2048, 512
FLOPS = 2 * K * H * S + 2 * H * R * S

F32 = mybir.dt.float32
BF16 = mybir.dt.bfloat16
I32 = mybir.dt.int32
U32 = mybir.dt.uint32
U16 = mybir.dt.uint16
U8 = mybir.dt.uint8
FP8X4 = mybir.dt.float8_e4m3fn_x4
ALU = mybir.AluOpType
ACT = mybir.ActivationFunctionType

P = 128
PACK = 4
D = 4
V = S // D
HALF = R // 2
FLOOR = 0.05
EXP_PAIR = 0x7F807F80


def tile_picked_ylabel_lin_p_kernel(tc, x_words, x_scales, w1, v_words, v_scales, offs, cand, out):
    nc = tc.nc
    with ExitStack() as ctx:
        keep = ctx.enter_context(tc.tile_pool(name="keep", bufs=1))
        psum = ctx.enter_context(tc.psum_pool(name="psum", bufs=1))

        offs_sb = keep.tile([P, S // 16], U16, name="offs_sb")
        cand_sb = keep.tile([P, R // 16], U16, name="cand_sb")
        x_tab = keep.tile([P, T], U32, name="x_tab", align_bytes=64)
        xs_tab = keep.tile([P, T], U8, name="xs_tab", align_bytes=64)
        v_tab = keep.tile([P, G], U32, name="v_tab", tag="v_then_h", align_bytes=64)
        vs_tab = keep.tile([P, G], U8, name="vs_tab", align_bytes=64)
        w_raw = [keep.tile([P, PACK, H // 2], F32, name=f"w_raw{u}", align_bytes=64) for u in range(2)]
        ident = keep.tile([P, P], F32, name="ident", align_bytes=64)
        one = keep.tile([P, 1], F32, name="one")
        warm = keep.tile([P, 1], F32, name="warm")

        nc.gpsimd.memset(xs_tab[:].bitcast(I32), 0)
        nc.vector.memset(one[:], 1.0)
        nc.gpsimd.memset(vs_tab[:].bitcast(I32), 0)

        w_rows = w1.rearrange("(p j) c -> p j c", j=PACK)
        nc.scalar.dma_start(w_raw[0][:], w_rows[:, :, 0 : H // 2])
        nc.sync.dma_start(offs_sb[:], offs)
        for q in range(4):
            nc.sync.dma_start(xs_tab[32 * q : 32 * q + 4, :].bitcast(I32), x_scales[0, 4 * q : 4 * q + 4, :].bitcast(I32))
        nc.sync.dma_start(w_raw[1][:], w_rows[:, :, H // 2 : H])
        nc.sync.dma_start(x_tab[:].bitcast(I32), x_words[0].rearrange("p n t -> p (n t)").bitcast(I32))
        nc.sync.dma_start(cand_sb[:], cand)
        for q in range(4):
            nc.sync.dma_start(vs_tab[32 * q : 32 * q + 4, :].bitcast(I32), v_scales[0, 4 * q : 4 * q + 4, :].bitcast(I32))
        nc.sync.dma_start(v_tab[:].bitcast(I32), v_words[0].rearrange("p n t -> p (n t)").bitcast(I32))
        make_identity(nc, ident[:])
        nc.scalar.activation(warm[:], one[:], ACT.Sqrt)

        xsg = keep.tile([P, S], U8, name="xsg", align_bytes=64)
        nc.vector.tensor_copy(xsg[:], xs_tab[:].indirect(offs_sb[:]))

        w_bf = keep.tile([P, PACK, P, PACK], BF16, name="w_bf", tag="w_then_x", align_bytes=64)
        for m0, m1, engine_copy in ((0, 64, nc.scalar.copy), (64, 80, nc.scalar.copy), (80, 128, nc.vector.tensor_copy)):
            u = m0 // 64
            dst = w_bf[:, :, m0:m1, :].rearrange("p t m j -> p m j t")
            src = w_raw[u][:].rearrange("p j (m t) -> p m j t", t=PACK)[:, m0 - 64 * u : m1 - 64 * u, :, :]
            engine_copy(dst, src)
        wq = keep.tile([P, H], U32, name="wq", align_bytes=64)
        wsq = keep.tile([P, H], U8, name="wsq", align_bytes=64)
        nc.vector.quantize_mx(out=wq[:].bitcast(FP8X4), scales=wsq[:], in_=w_bf[:].rearrange("p t m j -> p (t m j)"))

        xg_first = keep.tile([P, P], U32, name="xg_first", align_bytes=64)
        xg_rest = keep.tile([P, S - P], U32, name="xg_rest", tag="w_then_x", align_bytes=64)
        h_bf = keep.tile([P, D, V, PACK], BF16, name="h_bf", tag="h_then_vs", align_bytes=64)
        for c in range(4):
            hb = psum.tile([P, PACK, P], F32, name=f"hb{c}", tag=f"low{c}")
            cols = slice(c * P, (c + 1) * P)
            xg = xg_first[:] if c == 0 else xg_rest[:, (c - 1) * P : c * P]
            nc.vector.tensor_copy(xg, x_tab[:].indirect(offs_sb[:, c * (P // 16) : (c + 1) * (P // 16)]))
            for t in range(PACK):
                ch = slice(t * P, (t + 1) * P)
                nc.tensor.matmul_mx(out=hb[:, t, :], lhsT=wq[:, ch].bitcast(FP8X4), lhsT_scale=wsq[:, ch],
                                    rhs=xg.bitcast(FP8X4), rhs_scale=xsg[:, cols], start=True, stop=True)
            nc.scalar.copy(h_bf[:, :, 32 * c : 32 * (c + 1), :], hb[:].rearrange("p t (v d) -> p d v t", d=D))

        vsg = [keep.tile([P, HALF], U8, name="vsg0", align_bytes=64)]
        nc.vector.tensor_copy(vsg[0][:], vs_tab[:].indirect(cand_sb[:, 0 : HALF // 16]))
        vg = keep.tile([P, R], U32, name="vg", align_bytes=64)
        nc.vector.tensor_copy(vg[:], v_tab[:].indirect(cand_sb[:]))
        hq = keep.tile([P, S], U32, name="hq", tag="v_then_h", align_bytes=64)
        hsq = keep.tile([P, S], U8, name="hsq", align_bytes=64)
        for e in (1, 0):
            us = slice(2 * e * V, (2 * e + 2) * V)
            nc.vector.quantize_mx(out=hq[:, us].bitcast(FP8X4), scales=hsq[:, us],
                                  in_=h_bf[:, 2 * e : 2 * e + 2, :, :].rearrange("p d v t -> p (d v t)"))

        vsg.append(keep.tile([P, HALF], U8, name="vsg1", tag="h_then_vs", align_bytes=64))
        nc.vector.tensor_copy(vsg[1][:], vs_tab[:].indirect(cand_sb[:, HALF // 16 : R // 16]))

        y = [[psum.tile([P, 2, HALF], F32, name=f"y{u}{e}", tag=f"y{u}{e}") for e in range(2)] for u in range(2)]
        pos = [keep.tile([P, D, HALF], F32, name=f"pos{u}", align_bytes=64) for u in range(2)]
        ratio = [keep.tile([P, D, HALF], F32, name=f"ratio{u}", align_bytes=64) for u in range(2)]
        rs = [keep.tile([P, D, HALF], F32, name=f"rs{u}", align_bytes=64) for u in range(2)]
        wt = [keep.tile([P, D, HALF], F32, name=f"wt{u}", align_bytes=64) for u in range(2)]
        wy = [keep.tile([P, D, HALF], F32, name=f"wy{u}", align_bytes=64) for u in range(2)]

        top2 = [keep.tile([P, 2, HALF], BF16, name=f"top2{u}", align_bytes=64) for u in range(2)]
        top = [keep.tile([P, HALF], BF16, name=f"top{u}", align_bytes=64) for u in range(2)]
        inv = [keep.tile([P, HALF], BF16, name=f"inv{u}", align_bytes=64) for u in range(2)]
        den2 = [keep.tile([P, 2, V], F32, name=f"den2{u}", align_bytes=64) for u in range(2)]
        rden = [keep.tile([P, 2, V], F32, name=f"rden{u}", align_bytes=64) for u in range(2)]
        den = {}
        num = {}

        def pair(e):
            return slice(2 * e, 2 * e + 2)

        def second_product(u):
            for d in (2, 3, 0, 1):
                us = slice(d * V, (d + 1) * V)
                nc.tensor.matmul_mx(out=y[u][d // 2][:, d % 2, :], lhsT=hq[:, us].bitcast(FP8X4), lhsT_scale=hsq[:, us],
                                    rhs=vg[:, u * HALF : (u + 1) * HALF].bitcast(FP8X4), rhs_scale=vsg[u][:], start=True, stop=True)

        def relu(u, e):
            nc.scalar.activation(pos[u][:, pair(e), :], y[u][e][:], ACT.Relu)

        def top_of_pairs(u):
            nc.vector.scalar_tensor_tensor(top2[u][:], y[u][0][:], FLOOR, pos[u][:, 2:4, :], ALU.max, ALU.max)

        def top_of_four(u):
            nc.vector.tensor_tensor(top[u][:], top2[u][:, 0, :], top2[u][:, 1, :], ALU.max)

        def inverse_scale(u):
            nc.vector.tensor_scalar(inv[u][:].bitcast(I32), top[u][:].bitcast(I32), EXP_PAIR, EXP_PAIR, ALU.bitwise_xor, ALU.bitwise_and)

        def normalise(u, e):
            nc.vector.scalar_tensor_tensor(ratio[u][:, pair(e), :], pos[u][:, pair(e), :], FLOOR,
                                           inv[u][:].unsqueeze(1).to_broadcast([P, 2, HALF]), ALU.add, ALU.mult)
            nc.scalar.activation(rs[u][:, pair(e), :], ratio[u][:, pair(e), :], ACT.Sqrt, scale=1.0 / 256)

        def add_turned(dst, src, b, ds, first, last):
            for d in ds:
                nc.tensor.matmul(dst, lhsT=src[:, d, b * P : (b + 1) * P], rhs=ident[:], is_transpose=True,
                                 start=first and d == ds[0], stop=last and d == ds[-1])

        def weight(u, e):
            nc.vector.tensor_tensor(wt[u][:, pair(e), :], ratio[u][:, pair(e), :], rs[u][:, pair(e), :], ALU.mult)
            for b in range(2):
                if e == 1:
                    den[u, b] = psum.tile([P, V], F32, name=f"den{u}{b}", tag=f"low{2 * u + b}")
                add_turned(den[u, b][:], wt[u], b, (2 * e, 2 * e + 1), e == 1, e == 0)

        def invert_total(u):
            for b in range(2):
                nc.scalar.activation(den2[u][:, b, :], den[u, b][:], ACT.Abs_reciprocal_sqrt)
            nc.scalar.activation(rden[u][:], den2[u][:], ACT.Square)

        def weighted(u, e, blocks):
            ts = slice(blocks[0] * P, (blocks[-1] + 1) * P)
            nc.vector.tensor_tensor(wy[u][:, pair(e), ts], wt[u][:, pair(e), ts], y[u][e][:, :, ts], ALU.mult)
            for b in blocks:
                if e == 1:
                    num[u, b] = psum.tile([P, V], F32, name=f"num{u}{b}", tag=f"low{2 * u + b}")
                add_turned(num[u, b][:], wy[u], b, (2 * e, 2 * e + 1), e == 1, e == 0)

        def finish(u, b):
            res = keep.tile([P, V], F32, name=f"res{u}{b}", align_bytes=64)
            nc.vector.tensor_tensor(res[:], num[u, b][:], rden[u][:, b, :], ALU.mult)
            r0 = u * HALF + b * P
            nc.sync.dma_start(out[r0 : r0 + P, :], res[:])

        second_product(0)
        second_product(1)
        relu(0, 1)
        relu(1, 1)
        top_of_pairs(0)
        relu(0, 0)
        top_of_four(0)
        top_of_pairs(1)
        relu(1, 0)
        inverse_scale(0)
        top_of_four(1)
        normalise(0, 1)
        inverse_scale(1)
        normalise(0, 0)
        normalise(1, 1)
        normalise(1, 0)
        weight(0, 1)
        weight(0, 0)
        invert_total(0)
        weight(1, 1)
        weight(1, 0)
        invert_total(1)
        weighted(0, 1, (0, 1))
        weighted(0, 0, (0, 1))
        weighted(1, 1, (0, 1))
        finish(0, 0)
        finish(0, 1)
        weighted(1, 0, (0,))
        weighted(1, 0, (1,))
        finish(1, 0)
        finish(1, 1)
